import numpy as np
import ml_dtypes


def mxq(x, axis, fmt="e4m3"):
    dtype, down = {"e4m3": (ml_dtypes.float8_e4m3fn, 7), "e5m2": (ml_dtypes.float8_e5m2, 14)}[fmt]
    v = np.moveaxis(np.asarray(x, np.float32).astype(ml_dtypes.bfloat16).astype(np.float64), axis, -1)
    blocks = v.reshape(v.shape[:-1] + (-1, 32))
    amax = np.abs(blocks).max(-1, keepdims=True)
    byte = np.maximum(np.where(amax > 0, np.frexp(amax)[1] - 1 + 127, 0) - down, 1)
    scale = np.exp2(byte - 127.0)
    codes = (blocks / scale).astype(np.float32).astype(dtype).astype(np.float64)
    return np.moveaxis((codes * scale).reshape(v.shape), -1, axis)


WIDE = False


def mx_kscale(k):
    if not WIDE:
        return np.ones(k)
    levels = np.array([30, -30])
    if k % 512:
        return np.exp2(np.random.permutation(np.resize(levels, k // 32))).repeat(32)
    a = np.empty((k // 512, 16))
    for p in range(k // 512):
        a[p, :8] = np.random.permutation(np.resize(levels, 8))
        for g in range(8):
            far = levels[np.abs(levels - a[p, g]) >= 10]
            a[p, g + 8] = far[np.random.randint(len(far))]
    return np.exp2(a.ravel()).repeat(32)


BF16 = ml_dtypes.bfloat16


def bf(x):
    return np.asarray(x, np.float32).astype(BF16)


def f64(x):
    return np.asarray(x).astype(np.float64)


M, K, P, D = 1024, 2048, 1024, 1024


def setup_inputs():
    t = mx_kscale(K)
    s = mx_kscale(P)
    sign = np.where(np.random.random((M, K)) < 0.25, -1.0, 1.0)
    return {
        "logits": bf(2.0 * np.random.standard_normal((M, K)) - sign),
        "sign": bf(sign),
        "b": bf(-1.0 + 0.3 * np.random.standard_normal(K)),
        "c": bf((1.0 + 0.1 * np.random.standard_normal(K)) * t),
        "text": bf(np.random.standard_normal((K, D)) / np.sqrt(D) / t[:, None]),
        "r": bf(np.random.standard_normal((M, P)) * s),
        "w": bf(np.random.standard_normal((P, D)) / np.sqrt(P) / s[:, None]),
    }


def reference(logits, sign, b, c, text, r, w):
    z = f64(sign)
    g = z / (1.0 + np.exp(-z * (f64(logits) + f64(b)))) * f64(c)
    return ((mxq(g, 1, "e5m2") @ mxq(f64(text), 0, "e4m3"))
            + (mxq(f64(r), 1, "e4m3") @ mxq(f64(w), 0, "e4m3")))

@@ -1,0 +1,311 @@
+from contextlib import ExitStack
+
+import concourse.mybir as mybir
+from concourse.masks import make_identity
+
+M, K, R, D = 1024, 2048, 1024, 1024
+FLOPS = 2 * M * D * (K + R)
+
+F32 = mybir.dt.float32
+BF16 = mybir.dt.bfloat16
+U32 = mybir.dt.uint32
+U8 = mybir.dt.uint8
+E4M3 = mybir.dt.float8_e4m3fn_x4
+E5M2 = mybir.dt.float8_e5m2_x4
+ALU = mybir.AluOpType
+ACT = mybir.ActivationFunctionType
+
+P = 128
+PACK = 4
+K_PASS = P * PACK
+WORDS = K_PASS // 2
+N_TILE = 512
+HALVES = D // N_TILE
+TILES = 2
+ROWS = TILES * P
+BLOCKS = M // ROWS
+G_PASSES = K // K_PASS
+R_PASSES = R // K_PASS
+UNITS = BLOCKS * G_PASSES
+RUN = 4
+
+ORDER = (("g", 0), ("r", 0), ("g", 1), ("r", 1), ("g", 2), ("g", 3))
+B3_TICK = 4
+SIG_LATE = 0
+MODE = "rc"
+G_COLS = 256
+V_COLS = 96
+V_COLS1 = 96
+PH1 = 4
+S_PIECES = (2, 4, 6, 8, 10)
+OUT_V = (1, 3)
+LOADS = ["bc", "u0:1", "h0", "u1:2", "h1", "m1", "u2:3", "r0", "m2", "u3:4", "m3", "u4:5", "m4", "u5:6", "r1", "m5", "u6:8", "r2", "r3", "u8:12"]
+R_TICK = (1, 2, 3, 4, 5, 6, 7, 8)
+P_TICK = (-1, 0, 0, 1, 1, 2, 2, 3, 3, 4, 4, 5)
+
+
+def tile_siglip_image_gradient_s2_kernel(tc, logits, sign, b, c, text, r, w, out):
+    nc = tc.nc
+    with ExitStack() as ctx:
+        sb = ctx.enter_context(tc.tile_pool(name="sb", bufs=1))
+        ps = ctx.enter_context(tc.psum_pool(name="ps", bufs=1))
+        ctx.enter_context(tc.manual_schedule())
+
+        raw, lg, sg, rr, first = {}, {}, {}, {}, {}
+
+        def load_rows(dst, key, src, blk, cols, tag):
+            width = cols.stop - cols.start
+            t = sb.tile([P, TILES, width], BF16, name=tag, tag=tag)
+            nc.sync.dma_start(out=t[:], in_=src[blk * ROWS:(blk + 1) * ROWS, cols].rearrange("(a p) k -> p a k", p=P))
+            dst[key] = t
+
+        def load_units(n0, n1, tag_s, tag_l):
+            blk, g0 = divmod(n0, G_PASSES)
+            cols = slice(g0 * K_PASS, (g0 + n1 - n0) * K_PASS)
+            load_rows(sg, n0, sign, blk, cols, tag_s)
+            load_rows(lg, n0, logits, blk, cols, tag_l)
+            for n in range(n0, n1):
+                first[n] = n0
+
+        def moving_rows(q):
+            src, g = (w, ORDER[q][1]) if ORDER[q][0] == "r" else (text, ORDER[q][1])
+            return src[g * K_PASS:(g + 1) * K_PASS, :]
+
+        def load_moving(q):
+            t = sb.tile([P, PACK, D], BF16, name="raw%d" % q, tag="big%d" % q)
+            nc.sync.dma_start(out=t[:], in_=moving_rows(q).rearrange("(p t) d -> p t d", t=PACK))
+            for h in range(HALVES):
+                raw[q, h] = t[:, :, h * N_TILE:(h + 1) * N_TILE]
+
+        def load_moving_half(q, h):
+            t = sb.tile([P, PACK, N_TILE], BF16, name="rawh%d" % h, tag="rawh%d" % h)
+            nc.sync.dma_start(out=t[:], in_=moving_rows(q)[:, h * N_TILE:(h + 1) * N_TILE].rearrange("(p t) d -> p t d", t=PACK))
+            raw[q, h] = t[:]
+
+        ident = sb.tile([P, P], F32, name="ident")
+        make_identity(nc, ident[:])
+        warm = sb.tile([P, 1], F32, name="warm")
+        nc.vector.memset(warm[:], 0.0)
+        nc.scalar.activation(out=warm[:], in_=warm[:], func=ACT.Sigmoid)
+
+        bias = sb.tile([P, G_PASSES, PACK], BF16, name="bias")
+        gain = sb.tile([P, G_PASSES, PACK], BF16, name="gain")
+
+        for item in LOADS:
+            if item == "bc":
+                nc.sync.dma_start(out=bias[:], in_=b.rearrange("(g p t) -> p g t", p=P, t=PACK))
+                nc.sync.dma_start(out=gain[:], in_=c.rearrange("(g p t) -> p g t", p=P, t=PACK))
+            elif item[0] == "h":
+                load_moving_half(0, int(item[1:]))
+            elif item[0] == "m":
+                load_moving(int(item[1:]))
+            elif item[0] == "r":
+                load_rows(rr, int(item[1:]), r, int(item[1:]), slice(0, R), item)
+            else:
+                n0, n1 = item[1:].split(":")
+                load_units(int(n0), int(n1), "s" + item, "l" + item)
+
+        if MODE == "rc":
+            gain32 = sb.tile([P, G_PASSES, PACK], F32, name="gain32")
+            safe = sb.tile([P, G_PASSES, PACK], F32, name="safe")
+            inv = sb.tile([P, G_PASSES, PACK], F32, name="inv")
+            nc.vector.tensor_copy(out=gain32[:], in_=gain[:])
+            nc.vector.scalar_tensor_tensor(out=safe[:], in0=gain[:], scalar=0.0, in1=gain[:], op0=ALU.is_equal, op1=ALU.add)
+            nc.vector.reciprocal(out=inv[:], in_=safe[:])
+
+        def words_of(src, n):
+            return src[first[n]], n - first[n]
+
+        def transpose_pass(bank, rows, g):
+            for u in range(2):
+                for a in range(TILES):
+                    words = rows[:, a, :].bitcast(F32)
+                    nc.tensor.transpose(bank[:, u * ROWS + a * P:u * ROWS + (a + 1) * P],
+                                        words[:, g * WORDS + u:(g + 1) * WORDS:2], ident[:])
+
+        s_bank, l_bank, r_bank, s_words, v, sig, gt, gi, gq = {}, {}, {}, {}, {}, {}, {}, {}, {}
+        mi, mq, ri, rq, acc = {}, {}, {}, {}, {}
+        turn = [0]
+
+        def short_bank():
+            turn.append(0)
+            tag = "ts%d" % (len(turn) % (2 if MODE == "rc" else 1))
+            return ps.tile([P, 2 * ROWS], F32, name=tag, tag=tag)
+
+        def slot(ap, t):
+            return ap.bitcast(BF16).rearrange("p (u i e) -> p u e i", u=2, e=2)[:, t // 2, t % 2, :]
+
+        def t_unit(n):
+            short, held = (sg, lg) if MODE == "rc" else (lg, sg)
+            s_bank[n] = short_bank()
+            transpose_pass(s_bank[n], *words_of(short, n))
+            l_bank[n] = ps.tile([P, 2 * ROWS], F32, name="tl", tag="tl%d" % (n % (2 if MODE == "rc" else 3)))
+            transpose_pass(l_bank[n], *words_of(held, n))
+
+        def t_r(m):
+            r_bank[m] = short_bank()
+            transpose_pass(r_bank[m], rr[m // R_PASSES], m % R_PASSES)
+
+        def copy_s(n):
+            if MODE == "rc":
+                s_words[n] = sb.tile([P, PACK, ROWS], F32, name="sw", tag="sw%d" % (n % 3))
+                for t in range(PACK):
+                    nc.scalar.activation(out=s_words[n][:, t, :], in_=slot(s_bank[n][:], t), func=ACT.Copy,
+                                         scale=gain32[:, n % G_PASSES, t:t + 1])
+            else:
+                s_words[n] = sb.tile([P, 2 * ROWS], F32, name="sw", tag="sw%d" % (n % 2))
+                nc.scalar.copy(out=s_words[n][:], in_=s_bank[n][:])
+
+        def copy_r(m):
+            ri[m] = sb.tile([P, ROWS * PACK], BF16, name="ri", tag="ri%d" % (m % 2), align_bytes=64)
+            nc.scalar.copy(out=ri[m][:].bitcast(F32).rearrange("p (i u) -> p i u", u=2),
+                           in_=r_bank[m][:].rearrange("p (u i) -> p i u", u=2))
+
+        def quantize(src, width, dtype, tag):
+            codes = sb.tile([P, width], U32, name=tag + "c", tag=tag + "c", align_bytes=64)
+            scales = sb.tile([P, width], U8, name=tag + "s", tag=tag + "s", align_bytes=64)
+            nc.vector.quantize_mx(out=codes[:].bitcast(dtype), scales=scales[:], in_=src)
+            return codes, scales
+
+        def quant_r(m):
+            rq[m] = quantize(ri[m][:], ROWS, E4M3, "rq%d" % m)
+
+        def pre_act(n):
+            g = n % G_PASSES
+            v[n] = sb.tile([P, PACK, ROWS], F32, name="v", tag="v%d" % (n % 2))
+            for t in range(PACK):
+                if MODE == "rc":
+                    nc.vector.scalar_tensor_tensor(out=v[n][:, t, :], in0=slot(l_bank[n][:], t), scalar=bias[:, g, t:t + 1],
+                                                   in1=s_words[n][:, t, :], op0=ALU.add, op1=ALU.mult)
+                else:
+                    nc.vector.scalar_tensor_tensor(out=v[n][:, t, :], in0=slot(s_words[n][:], t), scalar=bias[:, g, t:t + 1],
+                                                   in1=slot(l_bank[n][:], t), op0=ALU.add, op1=ALU.mult)
+
+        def sigmoid(n):
+            sig[n] = sb.tile([P, PACK, ROWS], F32, name="sig", tag="sig%d" % (n % 2))
+            if MODE == "rc":
+                for t in range(PACK):
+                    nc.scalar.activation(out=sig[n][:, t, :], in_=v[n][:, t, :], func=ACT.Sigmoid,
+                                         scale=inv[:, n % G_PASSES, t:t + 1])
+            else:
+                nc.scalar.activation(out=sig[n][:], in_=v[n][:], func=ACT.Sigmoid)
+
+        def post_act(n):
+            g = n % G_PASSES
+            if MODE == "rc":
+                gi[n] = sb.tile([P, ROWS * PACK], BF16, name="gi", tag="gi%d" % (n % 2), align_bytes=64)
+                nc.vector.tensor_tensor(out=gi[n][:].rearrange("p (x i t) -> p x t i", i=2, t=PACK),
+                                        in0=sig[n][:].rearrange("p t (x i) -> p x t i", i=2),
+                                        in1=s_words[n][:].rearrange("p t (x i) -> p x t i", i=2), op=ALU.mult)
+                return
+            gt[n] = sb.tile([P, PACK, ROWS], BF16, name="gt", tag="gt%d" % (n % 2))
+            for t in range(PACK):
+                nc.vector.scalar_tensor_tensor(out=gt[n][:, t, :], in0=sig[n][:, t, :], scalar=gain[:, g, t:t + 1],
+                                               in1=slot(l_bank[n][:], t), op0=ALU.mult, op1=ALU.mult)
+
+        def inter_g_g(n):
+            gi[n] = sb.tile([P, ROWS * PACK], BF16, name="gi", tag="gi", align_bytes=64)
+            nc.gpsimd.tensor_scalar(out=gi[n][:, :G_COLS * PACK].rearrange("p (i t) -> p i t", t=PACK),
+                                    in0=gt[n][:, :, :G_COLS].rearrange("p t i -> p i t"),
+                                    scalar1=1.0, scalar2=0.0, op0=ALU.mult, op1=ALU.add)
+            if G_COLS < ROWS:
+                interleave(nc.scalar.copy, gi[n][:], gt[n][:], slice(G_COLS, ROWS))
+
+        def interleave(copy, dst, src, cols):
+            copy(out=dst.rearrange("p (x i t) -> p x t i", i=RUN, t=PACK)[:, cols.start // RUN:cols.stop // RUN],
+                 in_=src[:, :, cols].rearrange("p t (x i) -> p x t i", i=RUN))
+
+        def v_cols(n):
+            return V_COLS1 if n < PH1 else V_COLS
+
+        def inter_g_v(n):
+            gi[n] = sb.tile([P, ROWS * PACK], BF16, name="gi", tag="gi%d" % (n % 3), align_bytes=64)
+            if v_cols(n) > 0:
+                interleave(nc.vector.tensor_copy, gi[n][:], gt[n][:], slice(0, v_cols(n)))
+
+        def inter_g_s(n):
+            if v_cols(n) < ROWS:
+                interleave(nc.scalar.copy, gi[n][:], gt[n][:], slice(v_cols(n), ROWS))
+
+        def quant_g(n):
+            gq[n] = quantize(gi[n][:], ROWS, E5M2, "gq%d" % (n % 3))
+
+        def inter_m(j):
+            mi[j] = sb.tile([P, N_TILE * PACK], BF16, name="mi", tag="mi%d" % (j % 4), align_bytes=64)
+            copy = nc.scalar.copy if j in S_PIECES else nc.vector.tensor_copy
+            interleave(copy, mi[j][:], raw[divmod(j, HALVES)], slice(0, N_TILE))
+
+        def quant_m(j):
+            mq[j] = quantize(mi[j][:], N_TILE, E4M3, "mq%d" % j)
+
+        def multiply(blk, q, stationary, dtype):
+            codes, scales = stationary
+            for h in range(HALVES):
+                for a in range(TILES):
+                    if q == 0:
+                        acc[a, h] = ps.tile([P, N_TILE], F32, name="acc", tag="acc%d%d" % (a, h))
+                    cols = slice(a * P, (a + 1) * P)
+                    nc.tensor.matmul_mx(out=acc[a, h][:], lhsT=codes[:, cols].bitcast(dtype), lhsT_scale=scales[:, cols],
+                                        rhs=mq[q * HALVES + h][0][:].bitcast(E4M3), rhs_scale=mq[q * HALVES + h][1][:],
+                                        start=(q == 0), stop=(q == R_PASSES + G_PASSES - 1))
+
+        def store(blk):
+            for h in range(HALVES):
+                for a in range(TILES):
+                    k = h * TILES + a
+                    res = sb.tile([P, N_TILE], F32, name="res", tag="res%d" % ((blk % 2) * 4 + k))
+                    on_v = k in OUT_V or (blk == BLOCKS - 1 and k % 2 == 1)
+                    copy = nc.vector.tensor_copy if on_v else nc.scalar.copy
+                    copy(out=res[:], in_=acc[a, h][:])
+                    row0 = blk * ROWS + a * P
+                    nc.sync.dma_start(out=out[row0:row0 + P, h * N_TILE:(h + 1) * N_TILE], in_=res[:])
+
+        def unit(n):
+            return 0 <= n < UNITS
+
+        pieces = HALVES * (R_PASSES + G_PASSES)
+        r_units = BLOCKS * R_PASSES
+        for tick in range(-1, UNITS + 4):
+            mine = [j for j in range(pieces) if P_TICK[j] == tick]
+            r_mine = [m for m in range(r_units) if R_TICK[m] == tick]
+            done = tick - 4
+            if unit(done) and done % G_PASSES == G_PASSES - 1:
+                store(done // G_PASSES)
+            if unit(tick + 1):
+                t_unit(tick + 1)
+                copy_s(tick + 1)
+            if unit(tick - 2) and MODE == "gp":
+                inter_g_g(tick - 2)
+            if unit(tick - 2) and MODE == "sv":
+                inter_g_s(tick - 2)
+            if unit(tick):
+                pre_act(tick)
+            n = tick - 3
+            if unit(n):
+                blk, g = divmod(n, G_PASSES)
+                q = ORDER.index(("g", g))
+                if q > 0 and ORDER[q - 1][0] == "r":
+                    multiply(blk, q - 1, rq[blk * R_PASSES + ORDER[q - 1][1]], E4M3)
+                multiply(blk, q, gq[n], E5M2)
+            for m in r_mine:
+                t_r(m)
+            if unit(tick):
+                sigmoid(tick)
+            if unit(tick - 1):
+                post_act(tick - 1)
+            for m in r_mine:
+                copy_r(m)
+            for j in mine:
+                inter_m(j)
+            if unit(tick - 1) and MODE == "sv":
+                inter_g_v(tick - 1)
+            for j in range(pieces):
+                if P_TICK[j] == tick - (1 if j in S_PIECES else 0):
+                    quant_m(j)
+            for m in range(r_units):
+                if R_TICK[m] == tick - 1:
+                    quant_r(m)
+            if unit(tick - 2):
+                quant_g(tick - 2)
+            if tick == B3_TICK:
+                load_units(12, 16, "big1", "big2")

@@ -26,22 +26,21 @@ ROWS = TILES * P
 BLOCKS = M // ROWS
 G_PASSES = K // K_PASS
 R_PASSES = R // K_PASS
-UNITS = BLOCKS * G_PASSES
 RUN = 4
 
-ORDER = (("g", 0), ("r", 0), ("g", 1), ("r", 1), ("g", 2), ("g", 3))
+ORDER = (("g", 0), ("g", 1), ("r", 0), ("g", 2), ("r", 1), ("g", 3))
 B3_TICK = 4
-SIG_LATE = 0
-MODE = "rc"
-G_COLS = 256
-V_COLS = 96
-V_COLS1 = 96
-PH1 = 4
-S_PIECES = (2, 4, 6, 8, 10)
-OUT_V = (1, 3)
-LOADS = ["bc", "u0:1", "h0", "u1:2", "h1", "m1", "u2:3", "r0", "m2", "u3:4", "m3", "u4:5", "m4", "u5:6", "r1", "m5", "u6:8", "r2", "r3", "u8:12"]
-R_TICK = (1, 2, 3, 4, 5, 6, 7, 8)
-P_TICK = (-1, 0, 0, 1, 1, 2, 2, 3, 3, 4, 4, 5)
+SPLIT = 3
+QG_FIRST = 1
+TAIL_SPLIT = 1
+S_COLS = 448
+S_FIRST = 1
+S_COLS0 = 256
+LOAD_STYLE = 0
+FINE = 2
+OUT_V = (0,)
+R_TICK = (0, 1, 2, 3, 6, 7, 10, 11)
+WARM = 1
 
 
 def tile_siglip_image_gradient_s2_kernel(tc, logits, sign, b, c, text, r, w, out):
@@ -51,25 +50,22 @@ def tile_siglip_image_gradient_s2_kernel(tc, logits, sign, b, c, text, r, w, out
         ps = ctx.enter_context(tc.psum_pool(name="ps", bufs=1))
         ctx.enter_context(tc.manual_schedule())
 
-        raw, lg, sg, rr, first = {}, {}, {}, {}, {}
+        raw, lg, sg, rr = {}, {}, {}, {}
 
-        def load_rows(dst, key, src, blk, cols, tag):
-            width = cols.stop - cols.start
-            t = sb.tile([P, TILES, width], BF16, name=tag, tag=tag)
+        def load_rows(src, blk, cols, tag):
+            t = sb.tile([P, TILES, cols.stop - cols.start], BF16, name=tag, tag=tag)
             nc.sync.dma_start(out=t[:], in_=src[blk * ROWS:(blk + 1) * ROWS, cols].rearrange("(a p) k -> p a k", p=P))
-            dst[key] = t
+            return t
 
-        def load_units(n0, n1, tag_s, tag_l):
+        def load_passes(dst, src, n0, n1, tag):
             blk, g0 = divmod(n0, G_PASSES)
-            cols = slice(g0 * K_PASS, (g0 + n1 - n0) * K_PASS)
-            load_rows(sg, n0, sign, blk, cols, tag_s)
-            load_rows(lg, n0, logits, blk, cols, tag_l)
+            t = load_rows(src, blk, slice(g0 * K_PASS, (g0 + n1 - n0) * K_PASS), tag)
             for n in range(n0, n1):
-                first[n] = n0
+                dst[divmod(n, G_PASSES)] = (t, n - n0)
 
         def moving_rows(q):
-            src, g = (w, ORDER[q][1]) if ORDER[q][0] == "r" else (text, ORDER[q][1])
-            return src[g * K_PASS:(g + 1) * K_PASS, :]
+            src = w if ORDER[q][0] == "r" else text
+            return src[ORDER[q][1] * K_PASS:(ORDER[q][1] + 1) * K_PASS, :]
 
         def load_moving(q):
             t = sb.tile([P, PACK, D], BF16, name="raw%d" % q, tag="big%d" % q)
@@ -84,80 +80,94 @@ def tile_siglip_image_gradient_s2_kernel(tc, logits, sign, b, c, text, r, w, out
 
         ident = sb.tile([P, P], F32, name="ident")
         make_identity(nc, ident[:])
-        warm = sb.tile([P, 1], F32, name="warm")
-        nc.vector.memset(warm[:], 0.0)
-        nc.scalar.activation(out=warm[:], in_=warm[:], func=ACT.Sigmoid)
+        if WARM:
+            warm = sb.tile([P, 1], F32, name="warm")
+            nc.vector.memset(warm[:], 0.0)
+            nc.scalar.activation(out=warm[:], in_=warm[:], func=ACT.Sigmoid)
 
         bias = sb.tile([P, G_PASSES, PACK], BF16, name="bias")
         gain = sb.tile([P, G_PASSES, PACK], BF16, name="gain")
 
-        for item in LOADS:
-            if item == "bc":
-                nc.sync.dma_start(out=bias[:], in_=b.rearrange("(g p t) -> p g t", p=P, t=PACK))
-                nc.sync.dma_start(out=gain[:], in_=c.rearrange("(g p t) -> p g t", p=P, t=PACK))
-            elif item[0] == "h":
-                load_moving_half(0, int(item[1:]))
-            elif item[0] == "m":
-                load_moving(int(item[1:]))
-            elif item[0] == "r":
-                load_rows(rr, int(item[1:]), r, int(item[1:]), slice(0, R), item)
-            else:
-                n0, n1 = item[1:].split(":")
-                load_units(int(n0), int(n1), "s" + item, "l" + item)
+        def load_unit(n):
+            load_passes(sg, sign, n, n + 1, "s%d" % n)
+            load_passes(lg, logits, n, n + 1, "l%d" % n)
 
-        if MODE == "rc":
-            gain32 = sb.tile([P, G_PASSES, PACK], F32, name="gain32")
-            safe = sb.tile([P, G_PASSES, PACK], F32, name="safe")
-            inv = sb.tile([P, G_PASSES, PACK], F32, name="inv")
-            nc.vector.tensor_copy(out=gain32[:], in_=gain[:])
-            nc.vector.scalar_tensor_tensor(out=safe[:], in0=gain[:], scalar=0.0, in1=gain[:], op0=ALU.is_equal, op1=ALU.add)
-            nc.vector.reciprocal(out=inv[:], in_=safe[:])
+        load_moving_half(0, 0)
+        nc.sync.dma_start(out=gain[:], in_=c.rearrange("(g p t) -> p g t", p=P, t=PACK))
+        nc.sync.dma_start(out=bias[:], in_=b.rearrange("(g p t) -> p g t", p=P, t=PACK))
+        load_unit(0)
+        load_moving_half(0, 1)
+        for tick in range(BLOCKS * G_PASSES):
+            if tick + 1 < len(ORDER) and LOAD_STYLE == 0:
+                load_moving(tick + 1)
+            if tick + 1 < FINE * G_PASSES:
+                load_unit(tick + 1)
+            elif tick + 1 < (BLOCKS - 1) * G_PASSES and (tick + 1) % G_PASSES == 0:
+                load_passes(sg, sign, tick + 1, tick + 1 + G_PASSES, "sB%d" % tick)
+                load_passes(lg, logits, tick + 1, tick + 1 + G_PASSES, "lB%d" % tick)
+            if tick + 1 < len(ORDER) and LOAD_STYLE == 1:
+                load_moving(tick + 1)
+            for blk in range(BLOCKS):
+                if min(R_TICK[blk * R_PASSES], FINE * G_PASSES - 2) == tick:
+                    rr[blk] = load_rows(r, blk, slice(0, R), "r%d" % blk)
 
-        def words_of(src, n):
-            return src[first[n]], n - first[n]
+        gain32 = sb.tile([P, G_PASSES, PACK], F32, name="gain32")
+        safe = sb.tile([P, G_PASSES, PACK], F32, name="safe")
+        inv = sb.tile([P, G_PASSES, PACK], F32, name="inv")
+        nc.vector.tensor_copy(out=gain32[:], in_=gain[:])
+        nc.vector.scalar_tensor_tensor(out=safe[:], in0=gain[:], scalar=0.0, in1=gain[:], op0=ALU.is_equal, op1=ALU.add)
+        nc.vector.reciprocal(out=inv[:], in_=safe[:])
 
-        def transpose_pass(bank, rows, g):
+        both = tuple(range(TILES))
+        units = []
+        for blk in range(BLOCKS):
+            for g in range(G_PASSES):
+                if blk * G_PASSES + g >= BLOCKS * G_PASSES - TAIL_SPLIT:
+                    units.extend([(blk, g, (a,)) for a in both])
+                else:
+                    units.append((blk, g, both))
+
+        def rows_of(n):
+            return len(units[n][2]) * P
+
+        def transpose_pass(bank, rows, g, tiles):
             for u in range(2):
-                for a in range(TILES):
+                for j, a in enumerate(tiles):
                     words = rows[:, a, :].bitcast(F32)
-                    nc.tensor.transpose(bank[:, u * ROWS + a * P:u * ROWS + (a + 1) * P],
-                                        words[:, g * WORDS + u:(g + 1) * WORDS:2], ident[:])
+                    col = (u * len(tiles) + j) * P
+                    nc.tensor.transpose(bank[:, col:col + P], words[:, g * WORDS + u:(g + 1) * WORDS:2], ident[:])
 
-        s_bank, l_bank, r_bank, s_words, v, sig, gt, gi, gq = {}, {}, {}, {}, {}, {}, {}, {}, {}
+        s_bank, l_bank, r_bank, sc, v, sig, gi, gq = {}, {}, {}, {}, {}, {}, {}, {}
         mi, mq, ri, rq, acc = {}, {}, {}, {}, {}
         turn = [0]
 
         def short_bank():
             turn.append(0)
-            tag = "ts%d" % (len(turn) % (2 if MODE == "rc" else 1))
+            tag = "ts%d" % (len(turn) % 2)
             return ps.tile([P, 2 * ROWS], F32, name=tag, tag=tag)
 
-        def slot(ap, t):
-            return ap.bitcast(BF16).rearrange("p (u i e) -> p u e i", u=2, e=2)[:, t // 2, t % 2, :]
+        def slot(bank, rows, t):
+            return bank[:, :2 * rows].bitcast(BF16).rearrange("p (u i e) -> p u e i", u=2, e=2)[:, t // 2, t % 2, :]
 
         def t_unit(n):
-            short, held = (sg, lg) if MODE == "rc" else (lg, sg)
+            blk, g, tiles = units[n]
             s_bank[n] = short_bank()
-            transpose_pass(s_bank[n], *words_of(short, n))
-            l_bank[n] = ps.tile([P, 2 * ROWS], F32, name="tl", tag="tl%d" % (n % (2 if MODE == "rc" else 3)))
-            transpose_pass(l_bank[n], *words_of(held, n))
+            transpose_pass(s_bank[n], *sg[blk, g], tiles)
+            l_bank[n] = ps.tile([P, 2 * ROWS], F32, name="tl", tag="tl%d" % (n % 2))
+            transpose_pass(l_bank[n], *lg[blk, g], tiles)
 
         def t_r(m):
             r_bank[m] = short_bank()
-            transpose_pass(r_bank[m], rr[m // R_PASSES], m % R_PASSES)
+            transpose_pass(r_bank[m], rr[m // R_PASSES], m % R_PASSES, both)
 
-        def copy_s(n):
-            if MODE == "rc":
-                s_words[n] = sb.tile([P, PACK, ROWS], F32, name="sw", tag="sw%d" % (n % 3))
-                for t in range(PACK):
-                    nc.scalar.activation(out=s_words[n][:, t, :], in_=slot(s_bank[n][:], t), func=ACT.Copy,
-                                         scale=gain32[:, n % G_PASSES, t:t + 1])
-            else:
-                s_words[n] = sb.tile([P, 2 * ROWS], F32, name="sw", tag="sw%d" % (n % 2))
-                nc.scalar.copy(out=s_words[n][:], in_=s_bank[n][:])
+        def scale_sign(n):
+            sc[n] = sb.tile([P, PACK, rows_of(n)], F32, name="sw", tag="sw%d" % (n % 3))
+            for t in range(PACK):
+                nc.scalar.activation(out=sc[n][:, t, :], in_=slot(s_bank[n], rows_of(n), t), func=ACT.Copy,
+                                     scale=gain32[:, units[n][1], t:t + 1])
 
         def copy_r(m):
-            ri[m] = sb.tile([P, ROWS * PACK], BF16, name="ri", tag="ri%d" % (m % 2), align_bytes=64)
+            ri[m] = sb.tile([P, ROWS * PACK], BF16, name="ri", tag="ri%d" % (m % 3), align_bytes=64)
             nc.scalar.copy(out=ri[m][:].bitcast(F32).rearrange("p (i u) -> p i u", u=2),
                            in_=r_bank[m][:].rearrange("p (u i) -> p i u", u=2))
 
@@ -170,142 +180,123 @@ def tile_siglip_image_gradient_s2_kernel(tc, logits, sign, b, c, text, r, w, out
         def quant_r(m):
             rq[m] = quantize(ri[m][:], ROWS, E4M3, "rq%d" % m)
 
-        def pre_act(n):
-            g = n % G_PASSES
-            v[n] = sb.tile([P, PACK, ROWS], F32, name="v", tag="v%d" % (n % 2))
-            for t in range(PACK):
-                if MODE == "rc":
-                    nc.vector.scalar_tensor_tensor(out=v[n][:, t, :], in0=slot(l_bank[n][:], t), scalar=bias[:, g, t:t + 1],
-                                                   in1=s_words[n][:, t, :], op0=ALU.add, op1=ALU.mult)
-                else:
-                    nc.vector.scalar_tensor_tensor(out=v[n][:, t, :], in0=slot(s_words[n][:], t), scalar=bias[:, g, t:t + 1],
-                                                   in1=slot(l_bank[n][:], t), op0=ALU.add, op1=ALU.mult)
+        def pre_act(n, slots):
+            if slots[0] == 0:
+                v[n] = sb.tile([P, PACK, rows_of(n)], F32, name="v", tag="v%d" % (n % 2))
+            for t in slots:
+                nc.vector.scalar_tensor_tensor(out=v[n][:, t, :], in0=slot(l_bank[n], rows_of(n), t),
+                                               scalar=bias[:, units[n][1], t:t + 1],
+                                               in1=sc[n][:, t, :], op0=ALU.add, op1=ALU.mult)
 
-        def sigmoid(n):
-            sig[n] = sb.tile([P, PACK, ROWS], F32, name="sig", tag="sig%d" % (n % 2))
-            if MODE == "rc":
-                for t in range(PACK):
-                    nc.scalar.activation(out=sig[n][:, t, :], in_=v[n][:, t, :], func=ACT.Sigmoid,
-                                         scale=inv[:, n % G_PASSES, t:t + 1])
-            else:
-                nc.scalar.activation(out=sig[n][:], in_=v[n][:], func=ACT.Sigmoid)
+        def sigmoid(n, slots):
+            if slots[0] == 0:
+                sig[n] = sb.tile([P, PACK, rows_of(n)], F32, name="sig", tag="sig%d" % (n % 2))
+            for t in slots:
+                nc.scalar.activation(out=sig[n][:, t, :], in_=v[n][:, t, :], func=ACT.Sigmoid,
+                                     scale=inv[:, units[n][1], t:t + 1])
 
         def post_act(n):
-            g = n % G_PASSES
-            if MODE == "rc":
-                gi[n] = sb.tile([P, ROWS * PACK], BF16, name="gi", tag="gi%d" % (n % 2), align_bytes=64)
-                nc.vector.tensor_tensor(out=gi[n][:].rearrange("p (x i t) -> p x t i", i=2, t=PACK),
-                                        in0=sig[n][:].rearrange("p t (x i) -> p x t i", i=2),
-                                        in1=s_words[n][:].rearrange("p t (x i) -> p x t i", i=2), op=ALU.mult)
-                return
-            gt[n] = sb.tile([P, PACK, ROWS], BF16, name="gt", tag="gt%d" % (n % 2))
-            for t in range(PACK):
-                nc.vector.scalar_tensor_tensor(out=gt[n][:, t, :], in0=sig[n][:, t, :], scalar=gain[:, g, t:t + 1],
-                                               in1=slot(l_bank[n][:], t), op0=ALU.mult, op1=ALU.mult)
-
-        def inter_g_g(n):
-            gi[n] = sb.tile([P, ROWS * PACK], BF16, name="gi", tag="gi", align_bytes=64)
-            nc.gpsimd.tensor_scalar(out=gi[n][:, :G_COLS * PACK].rearrange("p (i t) -> p i t", t=PACK),
-                                    in0=gt[n][:, :, :G_COLS].rearrange("p t i -> p i t"),
-                                    scalar1=1.0, scalar2=0.0, op0=ALU.mult, op1=ALU.add)
-            if G_COLS < ROWS:
-                interleave(nc.scalar.copy, gi[n][:], gt[n][:], slice(G_COLS, ROWS))
-
-        def interleave(copy, dst, src, cols):
-            copy(out=dst.rearrange("p (x i t) -> p x t i", i=RUN, t=PACK)[:, cols.start // RUN:cols.stop // RUN],
-                 in_=src[:, :, cols].rearrange("p t (x i) -> p x t i", i=RUN))
-
-        def v_cols(n):
-            return V_COLS1 if n < PH1 else V_COLS
-
-        def inter_g_v(n):
-            gi[n] = sb.tile([P, ROWS * PACK], BF16, name="gi", tag="gi%d" % (n % 3), align_bytes=64)
-            if v_cols(n) > 0:
-                interleave(nc.vector.tensor_copy, gi[n][:], gt[n][:], slice(0, v_cols(n)))
-
-        def inter_g_s(n):
-            if v_cols(n) < ROWS:
-                interleave(nc.scalar.copy, gi[n][:], gt[n][:], slice(v_cols(n), ROWS))
+            gi[n] = sb.tile([P, rows_of(n) * PACK], BF16, name="gi", tag="gi%d" % (n % 2), align_bytes=64)
+            nc.vector.tensor_tensor(out=gi[n][:].rearrange("p (x i t) -> p x t i", i=2, t=PACK),
+                                    in0=sig[n][:].rearrange("p t (x i) -> p x t i", i=2),
+                                    in1=sc[n][:].rearrange("p t (x i) -> p x t i", i=2), op=ALU.mult)
 
         def quant_g(n):
-            gq[n] = quantize(gi[n][:], ROWS, E5M2, "gq%d" % (n % 3))
+            gq[n] = quantize(gi[n][:], rows_of(n), E5M2, "gq%d" % (n % 3))
 
-        def inter_m(j):
-            mi[j] = sb.tile([P, N_TILE * PACK], BF16, name="mi", tag="mi%d" % (j % 4), align_bytes=64)
-            copy = nc.scalar.copy if j in S_PIECES else nc.vector.tensor_copy
-            interleave(copy, mi[j][:], raw[divmod(j, HALVES)], slice(0, N_TILE))
+        def interleave(copy, j, c0, c1):
+            if j not in mi:
+                mi[j] = sb.tile([P, N_TILE * PACK], BF16, name="mi", tag="mi%d" % (j % 4), align_bytes=64)
+            copy(out=mi[j][:, c0 * PACK:c1 * PACK].rearrange("p (x i t) -> p x t i", i=RUN, t=PACK),
+                 in_=raw[divmod(j, HALVES)][:, :, c0:c1].rearrange("p t (x i) -> p x t i", i=RUN))
+
+        def s_cols(q):
+            return S_COLS0 if q == 0 else S_COLS
+
+        def inter_s(q):
+            interleave(nc.scalar.copy, q * HALVES + 1, N_TILE - s_cols(q), N_TILE)
+
+        def inter_v(q):
+            interleave(nc.vector.tensor_copy, q * HALVES, 0, N_TILE)
+            if s_cols(q) < N_TILE:
+                interleave(nc.vector.tensor_copy, q * HALVES + 1, 0, N_TILE - s_cols(q))
 
         def quant_m(j):
             mq[j] = quantize(mi[j][:], N_TILE, E4M3, "mq%d" % j)
 
-        def multiply(blk, q, stationary, dtype):
+        def multiply(q, stationary, dtype, tiles, held):
             codes, scales = stationary
             for h in range(HALVES):
-                for a in range(TILES):
+                for a in tiles:
                     if q == 0:
                         acc[a, h] = ps.tile([P, N_TILE], F32, name="acc", tag="acc%d%d" % (a, h))
-                    cols = slice(a * P, (a + 1) * P)
+                    j = held.index(a)
+                    cols = slice(j * P, (j + 1) * P)
                     nc.tensor.matmul_mx(out=acc[a, h][:], lhsT=codes[:, cols].bitcast(dtype), lhsT_scale=scales[:, cols],
                                         rhs=mq[q * HALVES + h][0][:].bitcast(E4M3), rhs_scale=mq[q * HALVES + h][1][:],
-                                        start=(q == 0), stop=(q == R_PASSES + G_PASSES - 1))
+                                        start=(q == 0), stop=(q == len(ORDER) - 1))
 
-        def store(blk):
+        def store(blk, tiles):
             for h in range(HALVES):
-                for a in range(TILES):
+                for a in tiles:
                     k = h * TILES + a
                     res = sb.tile([P, N_TILE], F32, name="res", tag="res%d" % ((blk % 2) * 4 + k))
-                    on_v = k in OUT_V or (blk == BLOCKS - 1 and k % 2 == 1)
+                    on_v = (h == 1 if len(tiles) == 1 else a == 1) if blk == BLOCKS - 1 else k in OUT_V
                     copy = nc.vector.tensor_copy if on_v else nc.scalar.copy
                     copy(out=res[:], in_=acc[a, h][:])
                     row0 = blk * ROWS + a * P
                     nc.sync.dma_start(out=out[row0:row0 + P, h * N_TILE:(h + 1) * N_TILE], in_=res[:])
 
         def unit(n):
-            return 0 <= n < UNITS
+            return 0 <= n < len(units)
 
-        pieces = HALVES * (R_PASSES + G_PASSES)
         r_units = BLOCKS * R_PASSES
-        for tick in range(-1, UNITS + 4):
-            mine = [j for j in range(pieces) if P_TICK[j] == tick]
+        early, late = tuple(range(SPLIT)), tuple(range(SPLIT, PACK))
+        for tick in range(-1, len(units) + 3):
+            q_mine = tick + 1 if tick + 1 < len(ORDER) else None
             r_mine = [m for m in range(r_units) if R_TICK[m] == tick]
-            done = tick - 4
-            if unit(done) and done % G_PASSES == G_PASSES - 1:
-                store(done // G_PASSES)
+            done = tick - 3
+            if unit(done) and units[done][1] == G_PASSES - 1:
+                store(units[done][0], units[done][2])
             if unit(tick + 1):
                 t_unit(tick + 1)
-                copy_s(tick + 1)
-            if unit(tick - 2) and MODE == "gp":
-                inter_g_g(tick - 2)
-            if unit(tick - 2) and MODE == "sv":
-                inter_g_s(tick - 2)
             if unit(tick):
-                pre_act(tick)
-            n = tick - 3
+                pre_act(tick, early)
+            if q_mine is not None and S_FIRST and tick >= 0:
+                inter_s(q_mine)
+            if unit(tick + 1):
+                scale_sign(tick + 1)
+            n = tick - 2
             if unit(n):
-                blk, g = divmod(n, G_PASSES)
+                blk, g, tiles = units[n]
                 q = ORDER.index(("g", g))
                 if q > 0 and ORDER[q - 1][0] == "r":
-                    multiply(blk, q - 1, rq[blk * R_PASSES + ORDER[q - 1][1]], E4M3)
-                multiply(blk, q, gq[n], E5M2)
-            for m in r_mine:
-                t_r(m)
+                    multiply(q - 1, rq[blk * R_PASSES + ORDER[q - 1][1]], E4M3, tiles, both)
+                multiply(q, gq[n], E5M2, tiles, tiles)
             if unit(tick):
-                sigmoid(tick)
+                sigmoid(tick, early)
             if unit(tick - 1):
                 post_act(tick - 1)
+            if unit(tick) and late:
+                pre_act(tick, late)
+                sigmoid(tick, late)
+            if unit(tick - 1) and QG_FIRST:
+                quant_g(tick - 1)
             for m in r_mine:
+                t_r(m)
                 copy_r(m)
-            for j in mine:
-                inter_m(j)
-            if unit(tick - 1) and MODE == "sv":
-                inter_g_v(tick - 1)
-            for j in range(pieces):
-                if P_TICK[j] == tick - (1 if j in S_PIECES else 0):
-                    quant_m(j)
+            if q_mine is not None:
+                if not S_FIRST or tick < 0:
+                    inter_s(q_mine)
+                inter_v(q_mine)
+                quant_m(q_mine * HALVES)
             for m in range(r_units):
                 if R_TICK[m] == tick - 1:
                     quant_r(m)
-            if unit(tick - 2):
-                quant_g(tick - 2)
+            if q_mine is not None:
+                quant_m(q_mine * HALVES + 1)
+            if unit(tick - 1) and not QG_FIRST:
+                quant_g(tick - 1)
             if tick == B3_TICK:
-                load_units(12, 16, "big1", "big2")
+                load_passes(sg, sign, 12, 16, "big1")
+                load_passes(lg, logits, 12, 16, "big2")

@@ -16,9 +16,9 @@ ALU = mybir.AluOpType
 ACT = mybir.ActivationFunctionType
 
 P = 128
-PACK = 4
-K_PASS = P * PACK
-WORDS = K_PASS // 2
+SLOTS = 4
+K_PASS = P * SLOTS
+PAIRS = K_PASS // 2
 N_TILE = 512
 HALVES = D // N_TILE
 TILES = 2
@@ -26,21 +26,15 @@ ROWS = TILES * P
 BLOCKS = M // ROWS
 G_PASSES = K // K_PASS
 R_PASSES = R // K_PASS
-RUN = 4
+TINY = 2.0 ** -100
 
-ORDER = (("g", 0), ("g", 1), ("r", 0), ("g", 2), ("r", 1), ("g", 3))
-B3_TICK = 4
-SPLIT = 3
-QG_FIRST = 1
-TAIL_SPLIT = 1
-S_COLS = 448
-S_FIRST = 1
-S_COLS0 = 256
-LOAD_STYLE = 0
-FINE = 2
-OUT_V = (0,)
-R_TICK = (0, 1, 2, 3, 6, 7, 10, 11)
-WARM = 1
+ROUNDS = [[("r", g)] * (g < R_PASSES) + [("g", g)] for g in range(G_PASSES)]
+PASSES = [key for keys in ROUNDS for key in keys]
+
+S_COLS = 416
+S_COLS_FIRST = 256
+EARLY_SLOTS = 3
+FINE_BLOCKS = 2
 
 
 def tile_siglip_image_gradient_s2_kernel(tc, logits, sign, b, c, text, r, w, out):
@@ -50,253 +44,234 @@ def tile_siglip_image_gradient_s2_kernel(tc, logits, sign, b, c, text, r, w, out
         ps = ctx.enter_context(tc.psum_pool(name="ps", bufs=1))
         ctx.enter_context(tc.manual_schedule())
 
-        raw, lg, sg, rr = {}, {}, {}, {}
-
-        def load_rows(src, blk, cols, tag):
-            t = sb.tile([P, TILES, cols.stop - cols.start], BF16, name=tag, tag=tag)
-            nc.sync.dma_start(out=t[:], in_=src[blk * ROWS:(blk + 1) * ROWS, cols].rearrange("(a p) k -> p a k", p=P))
-            return t
-
-        def load_passes(dst, src, n0, n1, tag):
-            blk, g0 = divmod(n0, G_PASSES)
-            t = load_rows(src, blk, slice(g0 * K_PASS, (g0 + n1 - n0) * K_PASS), tag)
-            for n in range(n0, n1):
-                dst[divmod(n, G_PASSES)] = (t, n - n0)
-
-        def moving_rows(q):
-            src = w if ORDER[q][0] == "r" else text
-            return src[ORDER[q][1] * K_PASS:(ORDER[q][1] + 1) * K_PASS, :]
-
-        def load_moving(q):
-            t = sb.tile([P, PACK, D], BF16, name="raw%d" % q, tag="big%d" % q)
-            nc.sync.dma_start(out=t[:], in_=moving_rows(q).rearrange("(p t) d -> p t d", t=PACK))
-            for h in range(HALVES):
-                raw[q, h] = t[:, :, h * N_TILE:(h + 1) * N_TILE]
-
-        def load_moving_half(q, h):
-            t = sb.tile([P, PACK, N_TILE], BF16, name="rawh%d" % h, tag="rawh%d" % h)
-            nc.sync.dma_start(out=t[:], in_=moving_rows(q)[:, h * N_TILE:(h + 1) * N_TILE].rearrange("(p t) d -> p t d", t=PACK))
-            raw[q, h] = t[:]
+        both = tuple(range(TILES))
+        units = [(blk, g, both) for blk in range(BLOCKS) for g in range(G_PASSES)][:-1]
+        units.extend([(BLOCKS - 1, G_PASSES - 1, (a,)) for a in both])
+        r_units = [(blk, g) for blk in range(BLOCKS) for g in range(R_PASSES)]
 
         ident = sb.tile([P, P], F32, name="ident")
         make_identity(nc, ident[:])
-        if WARM:
-            warm = sb.tile([P, 1], F32, name="warm")
-            nc.vector.memset(warm[:], 0.0)
-            nc.scalar.activation(out=warm[:], in_=warm[:], func=ACT.Sigmoid)
+        warm = sb.tile([P, 1], F32, name="warm")
+        nc.vector.memset(warm[:], 0.0)
+        nc.scalar.activation(out=warm[:], in_=warm[:], func=ACT.Sigmoid)
 
-        bias = sb.tile([P, G_PASSES, PACK], BF16, name="bias")
-        gain = sb.tile([P, G_PASSES, PACK], BF16, name="gain")
+        raw, sign_rows, logit_rows, r_rows = {}, {}, {}, {}
 
-        def load_unit(n):
-            load_passes(sg, sign, n, n + 1, "s%d" % n)
-            load_passes(lg, logits, n, n + 1, "l%d" % n)
+        def load_rows(src, blk, g0, g1, tag):
+            rows = sb.tile([P, TILES, (g1 - g0) * K_PASS], BF16, name=tag, tag=tag)
+            view = src[blk * ROWS:(blk + 1) * ROWS, g0 * K_PASS:g1 * K_PASS]
+            nc.sync.dma_start(out=rows[:], in_=view.rearrange("(a p) k -> p a k", p=P))
+            return {(blk, g): (rows, g - g0) for g in range(g0, g1)}
 
-        load_moving_half(0, 0)
-        nc.sync.dma_start(out=gain[:], in_=c.rearrange("(g p t) -> p g t", p=P, t=PACK))
-        nc.sync.dma_start(out=bias[:], in_=b.rearrange("(g p t) -> p g t", p=P, t=PACK))
-        load_unit(0)
-        load_moving_half(0, 1)
-        for tick in range(BLOCKS * G_PASSES):
-            if tick + 1 < len(ORDER) and LOAD_STYLE == 0:
-                load_moving(tick + 1)
-            if tick + 1 < FINE * G_PASSES:
-                load_unit(tick + 1)
-            elif tick + 1 < (BLOCKS - 1) * G_PASSES and (tick + 1) % G_PASSES == 0:
-                load_passes(sg, sign, tick + 1, tick + 1 + G_PASSES, "sB%d" % tick)
-                load_passes(lg, logits, tick + 1, tick + 1 + G_PASSES, "lB%d" % tick)
-            if tick + 1 < len(ORDER) and LOAD_STYLE == 1:
-                load_moving(tick + 1)
-            for blk in range(BLOCKS):
-                if min(R_TICK[blk * R_PASSES], FINE * G_PASSES - 2) == tick:
-                    rr[blk] = load_rows(r, blk, slice(0, R), "r%d" % blk)
+        def load_moving(q, h0, h1):
+            kind, g = PASSES[q]
+            src = w if kind == "r" else text
+            tag = "raw%d_%d" % (q, h0)
+            rows = sb.tile([P, SLOTS, (h1 - h0) * N_TILE], BF16, name=tag, tag=tag)
+            view = src[g * K_PASS:(g + 1) * K_PASS, h0 * N_TILE:h1 * N_TILE]
+            nc.sync.dma_start(out=rows[:], in_=view.rearrange("(p t) d -> p t d", t=SLOTS))
+            for h in range(h0, h1):
+                raw[q, h] = rows[:, :, (h - h0) * N_TILE:(h - h0 + 1) * N_TILE]
 
-        gain32 = sb.tile([P, G_PASSES, PACK], F32, name="gain32")
-        safe = sb.tile([P, G_PASSES, PACK], F32, name="safe")
-        inv = sb.tile([P, G_PASSES, PACK], F32, name="inv")
+        bias = sb.tile([P, G_PASSES, SLOTS], BF16, name="bias")
+        gain = sb.tile([P, G_PASSES, SLOTS], BF16, name="gain")
+        nc.sync.dma_start(out=gain[:], in_=c.rearrange("(g p t) -> p g t", p=P, t=SLOTS))
+        sign_rows.update(load_rows(sign, 0, 0, 1, "sign0"))
+        load_moving(0, 0, 1)
+        logit_rows.update(load_rows(logits, 0, 0, 1, "logit0"))
+        load_moving(0, 1, 2)
+        nc.sync.dma_start(out=bias[:], in_=b.rearrange("(g p t) -> p g t", p=P, t=SLOTS))
+        for n in range(1, FINE_BLOCKS * G_PASSES):
+            blk, g = divmod(n, G_PASSES)
+            if n < len(PASSES):
+                load_moving(n, 0, HALVES)
+            sign_rows.update(load_rows(sign, blk, g, g + 1, "sign%d" % n))
+            logit_rows.update(load_rows(logits, blk, g, g + 1, "logit%d" % n))
+            if (n - 1) % R_PASSES == 0:
+                r_rows.update(load_rows(r, (n - 1) // R_PASSES, 0, R_PASSES, "r%d" % n))
+        sign_rows.update(load_rows(sign, FINE_BLOCKS, 0, G_PASSES, "sign_block"))
+        logit_rows.update(load_rows(logits, FINE_BLOCKS, 0, G_PASSES, "logit_block"))
+
+        gain32 = sb.tile([P, G_PASSES, SLOTS], F32, name="gain32")
+        size = sb.tile([P, G_PASSES, SLOTS], F32, name="size")
+        safe = sb.tile([P, G_PASSES, SLOTS], F32, name="safe")
+        inv = sb.tile([P, G_PASSES, SLOTS], F32, name="inv")
         nc.vector.tensor_copy(out=gain32[:], in_=gain[:])
-        nc.vector.scalar_tensor_tensor(out=safe[:], in0=gain[:], scalar=0.0, in1=gain[:], op0=ALU.is_equal, op1=ALU.add)
-        nc.vector.reciprocal(out=inv[:], in_=safe[:])
 
-        both = tuple(range(TILES))
-        units = []
-        for blk in range(BLOCKS):
-            for g in range(G_PASSES):
-                if blk * G_PASSES + g >= BLOCKS * G_PASSES - TAIL_SPLIT:
-                    units.extend([(blk, g, (a,)) for a in both])
-                else:
-                    units.append((blk, g, both))
+        def invert_gain():
+            nc.vector.scalar_tensor_tensor(out=size[:], in0=gain[:], scalar=-1.0, in1=gain[:], op0=ALU.mult, op1=ALU.max)
+            nc.vector.scalar_tensor_tensor(out=safe[:], in0=size[:], scalar=TINY, in1=gain[:], op0=ALU.is_lt, op1=ALU.add)
+            nc.vector.reciprocal(out=inv[:], in_=safe[:])
 
-        def rows_of(n):
-            return len(units[n][2]) * P
+        sign_bank, logit_bank, sc, v, sig, g_side, g_mx = {}, {}, {}, {}, {}, {}, {}
+        r_side, r_mx, m_side, m_mx, acc, unit_of = {}, {}, {}, {}, {}, {}
+        short_uses = []
+
+        def short_bank():
+            short_uses.append(None)
+            tag = "short%d" % (len(short_uses) % 2)
+            return ps.tile([P, 2 * ROWS], F32, name=tag, tag=tag)
 
         def transpose_pass(bank, rows, g, tiles):
             for u in range(2):
                 for j, a in enumerate(tiles):
-                    words = rows[:, a, :].bitcast(F32)
+                    pairs = rows[:, a, :].bitcast(F32)
                     col = (u * len(tiles) + j) * P
-                    nc.tensor.transpose(bank[:, col:col + P], words[:, g * WORDS + u:(g + 1) * WORDS:2], ident[:])
+                    nc.tensor.transpose(bank[:, col:col + P], pairs[:, g * PAIRS + u:(g + 1) * PAIRS:2], ident[:])
 
-        s_bank, l_bank, r_bank, sc, v, sig, gi, gq = {}, {}, {}, {}, {}, {}, {}, {}
-        mi, mq, ri, rq, acc = {}, {}, {}, {}, {}
-        turn = [0]
-
-        def short_bank():
-            turn.append(0)
-            tag = "ts%d" % (len(turn) % 2)
-            return ps.tile([P, 2 * ROWS], F32, name=tag, tag=tag)
-
-        def slot(bank, rows, t):
+        def slot_of(bank, rows, t):
             return bank[:, :2 * rows].bitcast(BF16).rearrange("p (u i e) -> p u e i", u=2, e=2)[:, t // 2, t % 2, :]
 
-        def t_unit(n):
-            blk, g, tiles = units[n]
-            s_bank[n] = short_bank()
-            transpose_pass(s_bank[n], *sg[blk, g], tiles)
-            l_bank[n] = ps.tile([P, 2 * ROWS], F32, name="tl", tag="tl%d" % (n % 2))
-            transpose_pass(l_bank[n], *lg[blk, g], tiles)
+        def rows_of(n):
+            return len(units[n][2]) * P
 
-        def t_r(m):
-            r_bank[m] = short_bank()
-            transpose_pass(r_bank[m], rr[m // R_PASSES], m % R_PASSES, both)
+        def transpose_unit(n):
+            blk, g, tiles = units[n]
+            sign_bank[n] = short_bank()
+            transpose_pass(sign_bank[n], *sign_rows[blk, g], tiles)
+            logit_bank[n] = ps.tile([P, 2 * ROWS], F32, name="logit_bank", tag="logit_bank%d" % (n % 2))
+            transpose_pass(logit_bank[n], *logit_rows[blk, g], tiles)
 
         def scale_sign(n):
-            sc[n] = sb.tile([P, PACK, rows_of(n)], F32, name="sw", tag="sw%d" % (n % 3))
-            for t in range(PACK):
-                nc.scalar.activation(out=sc[n][:, t, :], in_=slot(s_bank[n], rows_of(n), t), func=ACT.Copy,
+            sc[n] = sb.tile([P, SLOTS, rows_of(n)], F32, name="sc", tag="sc%d" % (n % 3))
+            for t in range(SLOTS):
+                nc.scalar.activation(out=sc[n][:, t, :], in_=slot_of(sign_bank[n], rows_of(n), t), func=ACT.Copy,
                                      scale=gain32[:, units[n][1], t:t + 1])
 
-        def copy_r(m):
-            ri[m] = sb.tile([P, ROWS * PACK], BF16, name="ri", tag="ri%d" % (m % 3), align_bytes=64)
-            nc.scalar.copy(out=ri[m][:].bitcast(F32).rearrange("p (i u) -> p i u", u=2),
-                           in_=r_bank[m][:].rearrange("p (u i) -> p i u", u=2))
+        def pre_sigmoid(n, slots):
+            if n not in v:
+                v[n] = sb.tile([P, SLOTS, rows_of(n)], F32, name="v", tag="v%d" % (n % 2))
+            for t in slots:
+                nc.vector.scalar_tensor_tensor(out=v[n][:, t, :], in0=slot_of(logit_bank[n], rows_of(n), t),
+                                               scalar=bias[:, units[n][1], t:t + 1], in1=sc[n][:, t, :],
+                                               op0=ALU.add, op1=ALU.mult)
 
-        def quantize(src, width, dtype, tag):
+        def sigmoid(n, slots):
+            if n not in sig:
+                sig[n] = sb.tile([P, SLOTS, rows_of(n)], F32, name="sig", tag="sig%d" % (n % 2))
+            for t in slots:
+                nc.scalar.activation(out=sig[n][:, t, :], in_=v[n][:, t, :], func=ACT.Sigmoid,
+                                     scale=inv[:, units[n][1], t:t + 1])
+
+        def post_sigmoid(n):
+            g_side[n] = sb.tile([P, rows_of(n) * SLOTS], BF16, name="g_side", tag="g_side%d" % (n % 2), align_bytes=64)
+            nc.vector.tensor_tensor(out=g_side[n][:].rearrange("p (x i t) -> p x t i", i=2, t=SLOTS),
+                                    in0=sig[n][:].rearrange("p t (x i) -> p x t i", i=2),
+                                    in1=sc[n][:].rearrange("p t (x i) -> p x t i", i=2), op=ALU.mult)
+
+        def quantize(src, dtype, tag):
+            width = src.shape[1] // SLOTS
             codes = sb.tile([P, width], U32, name=tag + "c", tag=tag + "c", align_bytes=64)
             scales = sb.tile([P, width], U8, name=tag + "s", tag=tag + "s", align_bytes=64)
             nc.vector.quantize_mx(out=codes[:].bitcast(dtype), scales=scales[:], in_=src)
             return codes, scales
 
-        def quant_r(m):
-            rq[m] = quantize(ri[m][:], ROWS, E4M3, "rq%d" % m)
+        def quantize_g(n):
+            g_mx[n] = quantize(g_side[n][:], E5M2, "g_mx%d" % (n % 4))
+            for a in units[n][2]:
+                unit_of[units[n][0], units[n][1], a] = n
 
-        def pre_act(n, slots):
-            if slots[0] == 0:
-                v[n] = sb.tile([P, PACK, rows_of(n)], F32, name="v", tag="v%d" % (n % 2))
-            for t in slots:
-                nc.vector.scalar_tensor_tensor(out=v[n][:, t, :], in0=slot(l_bank[n], rows_of(n), t),
-                                               scalar=bias[:, units[n][1], t:t + 1],
-                                               in1=sc[n][:, t, :], op0=ALU.add, op1=ALU.mult)
+        def turn_r(m):
+            bank = short_bank()
+            transpose_pass(bank, *r_rows[r_units[m]], both)
+            r_side[m] = sb.tile([P, ROWS * SLOTS], BF16, name="r_side", tag="r_side%d" % (m % 3), align_bytes=64)
+            nc.scalar.copy(out=r_side[m][:].bitcast(F32).rearrange("p (i u) -> p i u", u=2),
+                           in_=bank[:].rearrange("p (u i) -> p i u", u=2))
 
-        def sigmoid(n, slots):
-            if slots[0] == 0:
-                sig[n] = sb.tile([P, PACK, rows_of(n)], F32, name="sig", tag="sig%d" % (n % 2))
-            for t in slots:
-                nc.scalar.activation(out=sig[n][:, t, :], in_=v[n][:, t, :], func=ACT.Sigmoid,
-                                     scale=inv[:, units[n][1], t:t + 1])
+        def interleave(copy, q, h, c0, c1):
+            if (q, h) not in m_side:
+                tag = "m_side%d" % ((q % 2) * HALVES + h)
+                m_side[q, h] = sb.tile([P, N_TILE * SLOTS], BF16, name=tag, tag=tag, align_bytes=64)
+            copy(out=m_side[q, h][:, c0 * SLOTS:c1 * SLOTS].rearrange("p (x i t) -> p x t i", i=4, t=SLOTS),
+                 in_=raw[q, h][:, :, c0:c1].rearrange("p t (x i) -> p x t i", i=4))
 
-        def post_act(n):
-            gi[n] = sb.tile([P, rows_of(n) * PACK], BF16, name="gi", tag="gi%d" % (n % 2), align_bytes=64)
-            nc.vector.tensor_tensor(out=gi[n][:].rearrange("p (x i t) -> p x t i", i=2, t=PACK),
-                                    in0=sig[n][:].rearrange("p t (x i) -> p x t i", i=2),
-                                    in1=sc[n][:].rearrange("p t (x i) -> p x t i", i=2), op=ALU.mult)
+        def interleave_scalar(q):
+            interleave(nc.scalar.copy, q, 1, N_TILE - (S_COLS if q else S_COLS_FIRST), N_TILE)
 
-        def quant_g(n):
-            gq[n] = quantize(gi[n][:], rows_of(n), E5M2, "gq%d" % (n % 3))
+        def interleave_vector(q):
+            interleave(nc.vector.tensor_copy, q, 0, 0, N_TILE)
+            interleave(nc.vector.tensor_copy, q, 1, 0, N_TILE - (S_COLS if q else S_COLS_FIRST))
 
-        def interleave(copy, j, c0, c1):
-            if j not in mi:
-                mi[j] = sb.tile([P, N_TILE * PACK], BF16, name="mi", tag="mi%d" % (j % 4), align_bytes=64)
-            copy(out=mi[j][:, c0 * PACK:c1 * PACK].rearrange("p (x i t) -> p x t i", i=RUN, t=PACK),
-                 in_=raw[divmod(j, HALVES)][:, :, c0:c1].rearrange("p t (x i) -> p x t i", i=RUN))
+        def quantize_moving(q, h):
+            m_mx[q, h] = quantize(m_side[q, h][:], E4M3, "m_mx%d_%d" % (q, h))
 
-        def s_cols(q):
-            return S_COLS0 if q == 0 else S_COLS
-
-        def inter_s(q):
-            interleave(nc.scalar.copy, q * HALVES + 1, N_TILE - s_cols(q), N_TILE)
-
-        def inter_v(q):
-            interleave(nc.vector.tensor_copy, q * HALVES, 0, N_TILE)
-            if s_cols(q) < N_TILE:
-                interleave(nc.vector.tensor_copy, q * HALVES + 1, 0, N_TILE - s_cols(q))
-
-        def quant_m(j):
-            mq[j] = quantize(mi[j][:], N_TILE, E4M3, "mq%d" % j)
-
-        def multiply(q, stationary, dtype, tiles, held):
-            codes, scales = stationary
-            for h in range(HALVES):
-                for a in tiles:
+        def multiply(blk, a, rnd):
+            for kind, g in ROUNDS[rnd]:
+                q = PASSES.index((kind, g))
+                if kind == "r":
+                    (codes, scales), dtype, j = r_mx[blk, g], E4M3, a
+                else:
+                    n = unit_of[blk, g, a]
+                    (codes, scales), dtype, j = g_mx[n], E5M2, units[n][2].index(a)
+                cols = slice(j * P, (j + 1) * P)
+                for h in range(HALVES):
                     if q == 0:
                         acc[a, h] = ps.tile([P, N_TILE], F32, name="acc", tag="acc%d%d" % (a, h))
-                    j = held.index(a)
-                    cols = slice(j * P, (j + 1) * P)
                     nc.tensor.matmul_mx(out=acc[a, h][:], lhsT=codes[:, cols].bitcast(dtype), lhsT_scale=scales[:, cols],
-                                        rhs=mq[q * HALVES + h][0][:].bitcast(E4M3), rhs_scale=mq[q * HALVES + h][1][:],
-                                        start=(q == 0), stop=(q == len(ORDER) - 1))
+                                        rhs=m_mx[q, h][0][:].bitcast(E4M3), rhs_scale=m_mx[q, h][1][:],
+                                        start=(q == 0), stop=(q == len(PASSES) - 1))
 
-        def store(blk, tiles):
+        def multiply_unit(n):
+            blk, g, tiles = units[n]
+            if 0 in tiles:
+                multiply(blk, 0, g)
+                if g > 0:
+                    multiply(blk, 1, g - 1)
+            if 1 in tiles and g == G_PASSES - 1:
+                multiply(blk, 1, g)
+
+        def store(blk, a):
             for h in range(HALVES):
-                for a in tiles:
-                    k = h * TILES + a
-                    res = sb.tile([P, N_TILE], F32, name="res", tag="res%d" % ((blk % 2) * 4 + k))
-                    on_v = (h == 1 if len(tiles) == 1 else a == 1) if blk == BLOCKS - 1 else k in OUT_V
-                    copy = nc.vector.tensor_copy if on_v else nc.scalar.copy
-                    copy(out=res[:], in_=acc[a, h][:])
-                    row0 = blk * ROWS + a * P
-                    nc.sync.dma_start(out=out[row0:row0 + P, h * N_TILE:(h + 1) * N_TILE], in_=res[:])
+                res = sb.tile([P, N_TILE], F32, name="res", tag="res%d%d%d" % (blk % 2, a, h))
+                on_vector = h == 1 if blk == BLOCKS - 1 else (a, h) == (0, 0)
+                copy = nc.vector.tensor_copy if on_vector else nc.scalar.copy
+                copy(out=res[:], in_=acc[a, h][:])
+                row0 = blk * ROWS + a * P
+                nc.sync.dma_start(out=out[row0:row0 + P, h * N_TILE:(h + 1) * N_TILE], in_=res[:])
 
-        def unit(n):
+        def is_unit(n):
             return 0 <= n < len(units)
 
-        r_units = BLOCKS * R_PASSES
-        early, late = tuple(range(SPLIT)), tuple(range(SPLIT, PACK))
-        for tick in range(-1, len(units) + 3):
-            q_mine = tick + 1 if tick + 1 < len(ORDER) else None
-            r_mine = [m for m in range(r_units) if R_TICK[m] == tick]
-            done = tick - 3
-            if unit(done) and units[done][1] == G_PASSES - 1:
-                store(units[done][0], units[done][2])
-            if unit(tick + 1):
-                t_unit(tick + 1)
-            if unit(tick):
-                pre_act(tick, early)
-            if q_mine is not None and S_FIRST and tick >= 0:
-                inter_s(q_mine)
-            if unit(tick + 1):
-                scale_sign(tick + 1)
-            n = tick - 2
-            if unit(n):
-                blk, g, tiles = units[n]
-                q = ORDER.index(("g", g))
-                if q > 0 and ORDER[q - 1][0] == "r":
-                    multiply(q - 1, rq[blk * R_PASSES + ORDER[q - 1][1]], E4M3, tiles, both)
-                multiply(q, gq[n], E5M2, tiles, tiles)
-            if unit(tick):
-                sigmoid(tick, early)
-            if unit(tick - 1):
-                post_act(tick - 1)
-            if unit(tick) and late:
-                pre_act(tick, late)
-                sigmoid(tick, late)
-            if unit(tick - 1) and QG_FIRST:
-                quant_g(tick - 1)
-            for m in r_mine:
-                t_r(m)
-                copy_r(m)
-            if q_mine is not None:
-                if not S_FIRST or tick < 0:
-                    inter_s(q_mine)
-                inter_v(q_mine)
-                quant_m(q_mine * HALVES)
-            for m in range(r_units):
-                if R_TICK[m] == tick - 1:
-                    quant_r(m)
-            if q_mine is not None:
-                quant_m(q_mine * HALVES + 1)
-            if unit(tick - 1) and not QG_FIRST:
-                quant_g(tick - 1)
-            if tick == B3_TICK:
-                load_passes(sg, sign, 12, 16, "big1")
-                load_passes(lg, logits, 12, 16, "big2")
+        early, late = range(EARLY_SLOTS), range(EARLY_SLOTS, SLOTS)
+        for step in range(-1, len(units) + 3):
+            q = step + 1
+            for a in both:
+                blk, rest = divmod(step - 2 - a, G_PASSES)
+                if rest == 0 and blk > 0:
+                    store(blk - 1, a)
+            if is_unit(step + 1):
+                transpose_unit(step + 1)
+            if is_unit(step):
+                pre_sigmoid(step, early)
+            if 0 < q < len(PASSES):
+                interleave_scalar(q)
+            if is_unit(step + 1):
+                scale_sign(step + 1)
+            if is_unit(step - 2):
+                multiply_unit(step - 2)
+            if is_unit(step):
+                sigmoid(step, early)
+            if is_unit(step - 1):
+                post_sigmoid(step - 1)
+            if is_unit(step):
+                pre_sigmoid(step, late)
+                sigmoid(step, late)
+            if is_unit(step - 1):
+                quantize_g(step - 1)
+            if 0 <= step < len(r_units):
+                turn_r(step)
+            if q == 0:
+                interleave_scalar(q)
+            if q < len(PASSES):
+                interleave_vector(q)
+            if q == 0:
+                invert_gain()
+            if q < len(PASSES):
+                quantize_moving(q, 0)
+            if 0 <= step - 1 < len(r_units):
+                r_mx[r_units[step - 1]] = quantize(r_side[step - 1][:], E4M3, "r_mx%d" % step)
+            if q < len(PASSES):
+                quantize_moving(q, 1)
+            if q == len(PASSES) - 1:
+                sign_rows.update(load_rows(sign, BLOCKS - 1, 0, G_PASSES, "raw1_0"))
+                logit_rows.update(load_rows(logits, BLOCKS - 1, 0, G_PASSES, "raw2_0"))

@@ -51,9 +51,6 @@ def tile_siglip_image_gradient_s2_kernel(tc, logits, sign, b, c, text, r, w, out
 
         ident = sb.tile([P, P], F32, name="ident")
         make_identity(nc, ident[:])
-        warm = sb.tile([P, 1], F32, name="warm")
-        nc.vector.memset(warm[:], 0.0)
-        nc.scalar.activation(out=warm[:], in_=warm[:], func=ACT.Sigmoid)
 
         raw, sign_rows, logit_rows, r_rows = {}, {}, {}, {}
 
@@ -75,12 +72,12 @@ def tile_siglip_image_gradient_s2_kernel(tc, logits, sign, b, c, text, r, w, out
 
         bias = sb.tile([P, G_PASSES, SLOTS], BF16, name="bias")
         gain = sb.tile([P, G_PASSES, SLOTS], BF16, name="gain")
-        nc.sync.dma_start(out=gain[:], in_=c.rearrange("(g p t) -> p g t", p=P, t=SLOTS))
+        nc.scalar.dma_start(out=gain[:], in_=c.rearrange("(g p t) -> p g t", p=P, t=SLOTS))
+        nc.scalar.dma_start(out=bias[:], in_=b.rearrange("(g p t) -> p g t", p=P, t=SLOTS))
         sign_rows.update(load_rows(sign, 0, 0, 1, "sign0"))
-        load_moving(0, 0, 1)
         logit_rows.update(load_rows(logits, 0, 0, 1, "logit0"))
-        load_moving(0, 1, 2)
-        nc.sync.dma_start(out=bias[:], in_=b.rearrange("(g p t) -> p g t", p=P, t=SLOTS))
+        for h in range(HALVES):
+            load_moving(0, h, h + 1)
         for n in range(1, FINE_BLOCKS * G_PASSES):
             blk, g = divmod(n, G_PASSES)
             if n < len(PASSES):
@@ -97,11 +94,9 @@ def tile_siglip_image_gradient_s2_kernel(tc, logits, sign, b, c, text, r, w, out
         safe = sb.tile([P, G_PASSES, SLOTS], F32, name="safe")
         inv = sb.tile([P, G_PASSES, SLOTS], F32, name="inv")
         nc.vector.tensor_copy(out=gain32[:], in_=gain[:])
-
-        def invert_gain():
-            nc.vector.scalar_tensor_tensor(out=size[:], in0=gain[:], scalar=-1.0, in1=gain[:], op0=ALU.mult, op1=ALU.max)
-            nc.vector.scalar_tensor_tensor(out=safe[:], in0=size[:], scalar=TINY, in1=gain[:], op0=ALU.is_lt, op1=ALU.add)
-            nc.vector.reciprocal(out=inv[:], in_=safe[:])
+        nc.vector.scalar_tensor_tensor(out=size[:], in0=gain[:], scalar=-1.0, in1=gain[:], op0=ALU.mult, op1=ALU.max)
+        nc.vector.scalar_tensor_tensor(out=safe[:], in0=size[:], scalar=TINY, in1=gain[:], op0=ALU.is_lt, op1=ALU.add)
+        nc.vector.reciprocal(out=inv[:], in_=safe[:])
 
         sign_bank, logit_bank, sc, v, sig, g_side, g_mx = {}, {}, {}, {}, {}, {}, {}
         r_side, r_mx, m_side, m_mx, acc, unit_of = {}, {}, {}, {}, {}, {}
@@ -135,8 +130,11 @@ def tile_siglip_image_gradient_s2_kernel(tc, logits, sign, b, c, text, r, w, out
         def scale_sign(n):
             sc[n] = sb.tile([P, SLOTS, rows_of(n)], F32, name="sc", tag="sc%d" % (n % 3))
             for t in range(SLOTS):
-                nc.scalar.activation(out=sc[n][:, t, :], in_=slot_of(sign_bank[n], rows_of(n), t), func=ACT.Copy,
-                                     scale=gain32[:, units[n][1], t:t + 1])
+                src, factor = slot_of(sign_bank[n], rows_of(n), t), gain32[:, units[n][1], t:t + 1]
+                if n == 0:
+                    nc.vector.tensor_scalar(out=sc[n][:, t, :], in0=src, scalar1=factor, scalar2=None, op0=ALU.mult)
+                else:
+                    nc.scalar.activation(out=sc[n][:, t, :], in_=src, func=ACT.Copy, scale=factor)
 
         def pre_sigmoid(n, slots):
             if n not in v:
@@ -232,8 +230,17 @@ def tile_siglip_image_gradient_s2_kernel(tc, logits, sign, b, c, text, r, w, out
         def is_unit(n):
             return 0 <= n < len(units)
 
+        transpose_unit(0)
+        scale_sign(0)
+        pre_sigmoid(0, range(SLOTS))
+        sigmoid(0, range(SLOTS))
+        interleave_scalar(0)
+        interleave_vector(0)
+        for h in range(HALVES):
+            quantize_moving(0, h)
+
         early, late = range(EARLY_SLOTS), range(EARLY_SLOTS, SLOTS)
-        for step in range(-1, len(units) + 3):
+        for step in range(len(units) + 3):
             q = step + 1
             for a in both:
                 blk, rest = divmod(step - 2 - a, G_PASSES)
@@ -241,32 +248,27 @@ def tile_siglip_image_gradient_s2_kernel(tc, logits, sign, b, c, text, r, w, out
                     store(blk - 1, a)
             if is_unit(step + 1):
                 transpose_unit(step + 1)
-            if is_unit(step):
+            if 0 < step < len(units):
                 pre_sigmoid(step, early)
-            if 0 < q < len(PASSES):
+            if q < len(PASSES):
                 interleave_scalar(q)
             if is_unit(step + 1):
                 scale_sign(step + 1)
             if is_unit(step - 2):
                 multiply_unit(step - 2)
-            if is_unit(step):
+            if 0 < step < len(units):
                 sigmoid(step, early)
             if is_unit(step - 1):
                 post_sigmoid(step - 1)
-            if is_unit(step):
+            if 0 < step < len(units):
                 pre_sigmoid(step, late)
                 sigmoid(step, late)
             if is_unit(step - 1):
                 quantize_g(step - 1)
-            if 0 <= step < len(r_units):
+            if step < len(r_units):
                 turn_r(step)
-            if q == 0:
-                interleave_scalar(q)
             if q < len(PASSES):
                 interleave_vector(q)
-            if q == 0:
-                invert_gain()
-            if q < len(PASSES):
                 quantize_moving(q, 0)
             if 0 <= step - 1 < len(r_units):
                 r_mx[r_units[step - 1]] = quantize(r_side[step - 1][:], E4M3, "r_mx%d" % step)

from contextlib import ExitStack

import concourse.mybir as mybir
from concourse.masks import make_identity

M, K, R, D = 1024, 2048, 1024, 1024
FLOPS = 2 * M * D * (K + R)

F32 = mybir.dt.float32
BF16 = mybir.dt.bfloat16
U32 = mybir.dt.uint32
U8 = mybir.dt.uint8
E4M3 = mybir.dt.float8_e4m3fn_x4
E5M2 = mybir.dt.float8_e5m2_x4
ALU = mybir.AluOpType
ACT = mybir.ActivationFunctionType

P = 128
SLOTS = 4
K_PASS = P * SLOTS
PAIRS = K_PASS // 2
N_TILE = 512
HALVES = D // N_TILE
TILES = 2
ROWS = TILES * P
BLOCKS = M // ROWS
G_PASSES = K // K_PASS
R_PASSES = R // K_PASS
TINY = 2.0 ** -100

ROUNDS = [[("r", g)] * (g < R_PASSES) + [("g", g)] for g in range(G_PASSES)]
PASSES = [key for keys in ROUNDS for key in keys]

S_COLS = 416
S_COLS_FIRST = 256
EARLY_SLOTS = 3
FINE_BLOCKS = 2


def tile_siglip_image_gradient_s2_kernel(tc, logits, sign, b, c, text, r, w, out):
    nc = tc.nc
    with ExitStack() as ctx:
        sb = ctx.enter_context(tc.tile_pool(name="sb", bufs=1))
        ps = ctx.enter_context(tc.psum_pool(name="ps", bufs=1))
        ctx.enter_context(tc.manual_schedule())

        both = tuple(range(TILES))
        units = [(blk, g, both) for blk in range(BLOCKS) for g in range(G_PASSES)][:-1]
        units.extend([(BLOCKS - 1, G_PASSES - 1, (a,)) for a in both])
        r_units = [(blk, g) for blk in range(BLOCKS) for g in range(R_PASSES)]

        ident = sb.tile([P, P], F32, name="ident")
        make_identity(nc, ident[:])

        raw, sign_rows, logit_rows, r_rows = {}, {}, {}, {}

        def load_rows(src, blk, g0, g1, tag):
            rows = sb.tile([P, TILES, (g1 - g0) * K_PASS], BF16, name=tag, tag=tag)
            view = src[blk * ROWS:(blk + 1) * ROWS, g0 * K_PASS:g1 * K_PASS]
            nc.sync.dma_start(out=rows[:], in_=view.rearrange("(a p) k -> p a k", p=P))
            return {(blk, g): (rows, g - g0) for g in range(g0, g1)}

        def load_moving(q, h0, h1):
            kind, g = PASSES[q]
            src = w if kind == "r" else text
            tag = "raw%d_%d" % (q, h0)
            rows = sb.tile([P, SLOTS, (h1 - h0) * N_TILE], BF16, name=tag, tag=tag)
            view = src[g * K_PASS:(g + 1) * K_PASS, h0 * N_TILE:h1 * N_TILE]
            nc.sync.dma_start(out=rows[:], in_=view.rearrange("(p t) d -> p t d", t=SLOTS))
            for h in range(h0, h1):
                raw[q, h] = rows[:, :, (h - h0) * N_TILE:(h - h0 + 1) * N_TILE]

        bias = sb.tile([P, G_PASSES, SLOTS], BF16, name="bias")
        gain = sb.tile([P, G_PASSES, SLOTS], BF16, name="gain")
        nc.scalar.dma_start(out=gain[:], in_=c.rearrange("(g p t) -> p g t", p=P, t=SLOTS))
        nc.scalar.dma_start(out=bias[:], in_=b.rearrange("(g p t) -> p g t", p=P, t=SLOTS))
        sign_rows.update(load_rows(sign, 0, 0, 1, "sign0"))
        logit_rows.update(load_rows(logits, 0, 0, 1, "logit0"))
        for h in range(HALVES):
            load_moving(0, h, h + 1)
        for n in range(1, FINE_BLOCKS * G_PASSES):
            blk, g = divmod(n, G_PASSES)
            if n < len(PASSES):
                load_moving(n, 0, HALVES)
            sign_rows.update(load_rows(sign, blk, g, g + 1, "sign%d" % n))
            logit_rows.update(load_rows(logits, blk, g, g + 1, "logit%d" % n))
            if (n - 1) % R_PASSES == 0:
                r_rows.update(load_rows(r, (n - 1) // R_PASSES, 0, R_PASSES, "r%d" % n))
        sign_rows.update(load_rows(sign, FINE_BLOCKS, 0, G_PASSES, "sign_block"))
        logit_rows.update(load_rows(logits, FINE_BLOCKS, 0, G_PASSES, "logit_block"))

        gain32 = sb.tile([P, G_PASSES, SLOTS], F32, name="gain32")
        size = sb.tile([P, G_PASSES, SLOTS], F32, name="size")
        safe = sb.tile([P, G_PASSES, SLOTS], F32, name="safe")
        inv = sb.tile([P, G_PASSES, SLOTS], F32, name="inv")
        nc.vector.tensor_copy(out=gain32[:], in_=gain[:])
        nc.vector.scalar_tensor_tensor(out=size[:], in0=gain[:], scalar=-1.0, in1=gain[:], op0=ALU.mult, op1=ALU.max)
        nc.vector.scalar_tensor_tensor(out=safe[:], in0=size[:], scalar=TINY, in1=gain[:], op0=ALU.is_lt, op1=ALU.add)
        nc.vector.reciprocal(out=inv[:], in_=safe[:])

        sign_bank, logit_bank, sc, v, sig, g_side, g_mx = {}, {}, {}, {}, {}, {}, {}
        r_side, r_mx, m_side, m_mx, acc, unit_of = {}, {}, {}, {}, {}, {}
        short_uses = []

        def short_bank():
            short_uses.append(None)
            tag = "short%d" % (len(short_uses) % 2)
            return ps.tile([P, 2 * ROWS], F32, name=tag, tag=tag)

        def transpose_pass(bank, rows, g, tiles):
            for u in range(2):
                for j, a in enumerate(tiles):
                    pairs = rows[:, a, :].bitcast(F32)
                    col = (u * len(tiles) + j) * P
                    nc.tensor.transpose(bank[:, col:col + P], pairs[:, g * PAIRS + u:(g + 1) * PAIRS:2], ident[:])

        def slot_of(bank, rows, t):
            return bank[:, :2 * rows].bitcast(BF16).rearrange("p (u i e) -> p u e i", u=2, e=2)[:, t // 2, t % 2, :]

        def rows_of(n):
            return len(units[n][2]) * P

        def transpose_unit(n):
            blk, g, tiles = units[n]
            sign_bank[n] = short_bank()
            transpose_pass(sign_bank[n], *sign_rows[blk, g], tiles)
            logit_bank[n] = ps.tile([P, 2 * ROWS], F32, name="logit_bank", tag="logit_bank%d" % (n % 2))
            transpose_pass(logit_bank[n], *logit_rows[blk, g], tiles)

        def scale_sign(n):
            sc[n] = sb.tile([P, SLOTS, rows_of(n)], F32, name="sc", tag="sc%d" % (n % 3))
            for t in range(SLOTS):
                src, factor = slot_of(sign_bank[n], rows_of(n), t), gain32[:, units[n][1], t:t + 1]
                if n == 0:
                    nc.vector.tensor_scalar(out=sc[n][:, t, :], in0=src, scalar1=factor, scalar2=None, op0=ALU.mult)
                else:
                    nc.scalar.activation(out=sc[n][:, t, :], in_=src, func=ACT.Copy, scale=factor)

        def pre_sigmoid(n, slots):
            if n not in v:
                v[n] = sb.tile([P, SLOTS, rows_of(n)], F32, name="v", tag="v%d" % (n % 2))
            for t in slots:
                nc.vector.scalar_tensor_tensor(out=v[n][:, t, :], in0=slot_of(logit_bank[n], rows_of(n), t),
                                               scalar=bias[:, units[n][1], t:t + 1], in1=sc[n][:, t, :],
                                               op0=ALU.add, op1=ALU.mult)

        def sigmoid(n, slots):
            if n not in sig:
                sig[n] = sb.tile([P, SLOTS, rows_of(n)], F32, name="sig", tag="sig%d" % (n % 2))
            for t in slots:
                nc.scalar.activation(out=sig[n][:, t, :], in_=v[n][:, t, :], func=ACT.Sigmoid,
                                     scale=inv[:, units[n][1], t:t + 1])

        def post_sigmoid(n):
            g_side[n] = sb.tile([P, rows_of(n) * SLOTS], BF16, name="g_side", tag="g_side%d" % (n % 2), align_bytes=64)
            nc.vector.tensor_tensor(out=g_side[n][:].rearrange("p (x i t) -> p x t i", i=2, t=SLOTS),
                                    in0=sig[n][:].rearrange("p t (x i) -> p x t i", i=2),
                                    in1=sc[n][:].rearrange("p t (x i) -> p x t i", i=2), op=ALU.mult)

        def quantize(src, dtype, tag):
            width = src.shape[1] // SLOTS
            codes = sb.tile([P, width], U32, name=tag + "c", tag=tag + "c", align_bytes=64)
            scales = sb.tile([P, width], U8, name=tag + "s", tag=tag + "s", align_bytes=64)
            nc.vector.quantize_mx(out=codes[:].bitcast(dtype), scales=scales[:], in_=src)
            return codes, scales

        def quantize_g(n):
            g_mx[n] = quantize(g_side[n][:], E5M2, "g_mx%d" % (n % 4))
            for a in units[n][2]:
                unit_of[units[n][0], units[n][1], a] = n

        def turn_r(m):
            bank = short_bank()
            transpose_pass(bank, *r_rows[r_units[m]], both)
            r_side[m] = sb.tile([P, ROWS * SLOTS], BF16, name="r_side", tag="r_side%d" % (m % 3), align_bytes=64)
            nc.scalar.copy(out=r_side[m][:].bitcast(F32).rearrange("p (i u) -> p i u", u=2),
                           in_=bank[:].rearrange("p (u i) -> p i u", u=2))

        def interleave(copy, q, h, c0, c1):
            if (q, h) not in m_side:
                tag = "m_side%d" % ((q % 2) * HALVES + h)
                m_side[q, h] = sb.tile([P, N_TILE * SLOTS], BF16, name=tag, tag=tag, align_bytes=64)
            copy(out=m_side[q, h][:, c0 * SLOTS:c1 * SLOTS].rearrange("p (x i t) -> p x t i", i=4, t=SLOTS),
                 in_=raw[q, h][:, :, c0:c1].rearrange("p t (x i) -> p x t i", i=4))

        def interleave_scalar(q):
            interleave(nc.scalar.copy, q, 1, N_TILE - (S_COLS if q else S_COLS_FIRST), N_TILE)

        def interleave_vector(q):
            interleave(nc.vector.tensor_copy, q, 0, 0, N_TILE)
            interleave(nc.vector.tensor_copy, q, 1, 0, N_TILE - (S_COLS if q else S_COLS_FIRST))

        def quantize_moving(q, h):
            m_mx[q, h] = quantize(m_side[q, h][:], E4M3, "m_mx%d_%d" % (q, h))

        def multiply(blk, a, rnd):
            for kind, g in ROUNDS[rnd]:
                q = PASSES.index((kind, g))
                if kind == "r":
                    (codes, scales), dtype, j = r_mx[blk, g], E4M3, a
                else:
                    n = unit_of[blk, g, a]
                    (codes, scales), dtype, j = g_mx[n], E5M2, units[n][2].index(a)
                cols = slice(j * P, (j + 1) * P)
                for h in range(HALVES):
                    if q == 0:
                        acc[a, h] = ps.tile([P, N_TILE], F32, name="acc", tag="acc%d%d" % (a, h))
                    nc.tensor.matmul_mx(out=acc[a, h][:], lhsT=codes[:, cols].bitcast(dtype), lhsT_scale=scales[:, cols],
                                        rhs=m_mx[q, h][0][:].bitcast(E4M3), rhs_scale=m_mx[q, h][1][:],
                                        start=(q == 0), stop=(q == len(PASSES) - 1))

        def multiply_unit(n):
            blk, g, tiles = units[n]
            if 0 in tiles:
                multiply(blk, 0, g)
                if g > 0:
                    multiply(blk, 1, g - 1)
            if 1 in tiles and g == G_PASSES - 1:
                multiply(blk, 1, g)

        def store(blk, a):
            for h in range(HALVES):
                res = sb.tile([P, N_TILE], F32, name="res", tag="res%d%d%d" % (blk % 2, a, h))
                on_vector = h == 1 if blk == BLOCKS - 1 else (a, h) == (0, 0)
                copy = nc.vector.tensor_copy if on_vector else nc.scalar.copy
                copy(out=res[:], in_=acc[a, h][:])
                row0 = blk * ROWS + a * P
                nc.sync.dma_start(out=out[row0:row0 + P, h * N_TILE:(h + 1) * N_TILE], in_=res[:])

        def is_unit(n):
            return 0 <= n < len(units)

        transpose_unit(0)
        scale_sign(0)
        pre_sigmoid(0, range(SLOTS))
        sigmoid(0, range(SLOTS))
        interleave_scalar(0)
        interleave_vector(0)
        for h in range(HALVES):
            quantize_moving(0, h)

        early, late = range(EARLY_SLOTS), range(EARLY_SLOTS, SLOTS)
        for step in range(len(units) + 3):
            q = step + 1
            for a in both:
                blk, rest = divmod(step - 2 - a, G_PASSES)
                if rest == 0 and blk > 0:
                    store(blk - 1, a)
            if is_unit(step + 1):
                transpose_unit(step + 1)
            if 0 < step < len(units):
                pre_sigmoid(step, early)
            if q < len(PASSES):
                interleave_scalar(q)
            if is_unit(step + 1):
                scale_sign(step + 1)
            if is_unit(step - 2):
                multiply_unit(step - 2)
            if 0 < step < len(units):
                sigmoid(step, early)
            if is_unit(step - 1):
                post_sigmoid(step - 1)
            if 0 < step < len(units):
                pre_sigmoid(step, late)
                sigmoid(step, late)
            if is_unit(step - 1):
                quantize_g(step - 1)
            if step < len(r_units):
                turn_r(step)
            if q < len(PASSES):
                interleave_vector(q)
                quantize_moving(q, 0)
            if 0 <= step - 1 < len(r_units):
                r_mx[r_units[step - 1]] = quantize(r_side[step - 1][:], E4M3, "r_mx%d" % step)
            if q < len(PASSES):
                quantize_moving(q, 1)
            if q == len(PASSES) - 1:
                sign_rows.update(load_rows(sign, BLOCKS - 1, 0, G_PASSES, "raw1_0"))
                logit_rows.update(load_rows(logits, BLOCKS - 1, 0, G_PASSES, "raw2_0"))
